import numpy as np
import ml_dtypes


def mxq(x, axis, fmt="e4m3"):
    dtype, down = {"e4m3": (ml_dtypes.float8_e4m3fn, 7), "e5m2": (ml_dtypes.float8_e5m2, 14)}[fmt]
    v = np.moveaxis(np.asarray(x, np.float32).astype(ml_dtypes.bfloat16).astype(np.float64), axis, -1)
    blocks = v.reshape(v.shape[:-1] + (-1, 32))
    amax = np.abs(blocks).max(-1, keepdims=True)
    byte = np.maximum(np.where(amax > 0, np.frexp(amax)[1] - 1 + 127, 0) - down, 1)
    scale = np.exp2(byte - 127.0)
    codes = (blocks / scale).astype(np.float32).astype(dtype).astype(np.float64)
    return np.moveaxis((codes * scale).reshape(v.shape), -1, axis)


WIDE = False


def mx_kscale(k, group=512):
    if not WIDE:
        return np.ones(k)
    levels = np.array([10, -10, 5, -5, 0])
    if group != 512:
        return np.exp2(np.random.permutation(np.resize(levels, k // group))).repeat(group)
    if k % 512:
        return np.exp2(np.random.permutation(np.resize(levels, k // 32))).repeat(32)
    a = np.empty((k // 512, 16))
    for p in range(k // 512):
        a[p, :8] = np.random.permutation(np.resize(levels, 8))
        for g in range(8):
            far = levels[np.abs(levels - a[p, g]) >= 10]
            a[p, g + 8] = far[np.random.randint(len(far))]
    return np.exp2(a.ravel()).repeat(32)


def f64(x):
    return np.asarray(x).astype(np.float64)


def softplus(v):
    return np.log(1.0 + np.exp(v))


G, D, M, O, N = 2, 256, 256, 256, 512


def sgn(shape):
    return np.random.uniform(0.5, 2.0, shape) * np.where(np.random.standard_normal(shape) < 0, -1.0, 1.0)


def setup_inputs():
    n = np.random.standard_normal
    s_d = mx_kscale(D, 0)
    s_m = mx_kscale(M, 0)
    return {
        "x": (n((G, D, N)) * s_d[:, None]).astype(np.float32),
        "w1": (n((G, D, M)) / np.sqrt(D) / s_d[:, None]).astype(np.float32),
        "w2": (n((G, D, M)) / np.sqrt(D) / s_d[:, None]).astype(np.float32),
        "re": (np.random.uniform(50.0, 200.0, (G, M, 1))).astype(np.float32),
        "hs": (sgn((G, M, 1)) * s_m[:, None]).astype(np.float32),
        "wo2": (n((G, M, O)) / np.sqrt(M) / s_m[:, None]).astype(np.float32),
        "ob": (0.5 * n((G, O, 1))).astype(np.float32),
        "osc": (np.random.uniform(0.5, 2.0, (G, O, 1))).astype(np.float32),
    }


def reference(x, w1, w2, re, hs, wo2, ob, osc):
    w1q = mxq(f64(w1), 1, "e4m3")
    xq = mxq(f64(x), 1, "e4m3")
    z1 = w1q.transpose(0, 2, 1) @ xq
    w2q = mxq(f64(w2), 1, "e4m3")
    z2 = w2q.transpose(0, 2, 1) @ xq
    p1 = softplus(z1)
    zs = np.sum(p1, axis=-1, keepdims=True) + f64(re)
    h = p1 / zs * np.tanh(z2) * 512.0
    hh = h * f64(hs)
    wo2q = mxq(f64(wo2), 1, "e4m3")
    hhq = mxq(hh, 1, "e4m3")
    y0 = wo2q.transpose(0, 2, 1) @ hhq
    y = np.tanh(y0 + f64(ob)) * f64(osc)
    return y

@@ -1,0 +1,209 @@
+from contextlib import ExitStack
+
+import concourse.mybir as mybir
+
+F32 = mybir.dt.float32
+BF16 = mybir.dt.bfloat16
+I32 = mybir.dt.int32
+U32 = mybir.dt.uint32
+U8 = mybir.dt.uint8
+FP8X4 = mybir.dt.float8_e4m3fn_x4
+ACT = mybir.ActivationFunctionType
+ALU = mybir.AluOpType
+
+G, K, N = 2, 256, 512
+P = 128
+PACK = 4
+ROWS = K // PACK
+TILES = K // P
+HALVES = 2
+HALF = N // HALVES
+MM_N = 128
+EXP_CAP = 2.0**60
+
+FLOPS = 3 * 2 * G * K * K * N
+
+
+def tile_rows_frowshare_kernel(tc, x, w1, w2, reserve, hs, wo2, ob, osc, out):
+    nc = tc.nc
+
+    with ExitStack() as ctx:
+        sb = ctx.enter_context(tc.tile_pool(name="sb", bufs=1))
+        ps = ctx.enter_context(tc.psum_pool(name="ps", bufs=1))
+        ctx.enter_context(tc.manual_schedule())
+
+        def load_rows(name, src):
+            raw = sb.tile([P, PACK, src.shape[2]], F32, name=name + "_raw", align_bytes=64)
+            nc.sync.dma_start(out=raw[:], in_=src)
+            return raw
+
+        def load_per_feature(name, src):
+            vec = sb.tile([P, G, 8], F32, name=name + "_sb")
+            nc.sync.dma_start(out=vec[:, :, 0:TILES], in_=src.rearrange("g (q t) o -> q g (t o)", t=TILES))
+            return vec
+
+        def packed_rows(src):
+            return src.rearrange("g (p j) c -> (g p) j c", j=PACK)
+
+        def quantize(name, grouped, width):
+            codes = sb.tile([P, width], U32, name=name + "_codes", align_bytes=64)
+            scales = sb.tile([P, width], U8, name=name + "_scales", align_bytes=64)
+            nc.vector.quantize_mx(out=codes[:].bitcast(FP8X4), scales=scales[:], in_=grouped[:])
+            return codes, scales
+
+        def group_weights(name, raw):
+            grouped = sb.tile([P, K * PACK], BF16, name=name + "_grouped", align_bytes=64)
+            nc.vector.tensor_copy(
+                out=grouped[:].rearrange("p (t q j) -> p t q j", t=TILES, j=PACK),
+                in_=raw[:].rearrange("p j (q t) -> p t q j", t=TILES),
+            )
+            return grouped
+
+        def multiply(acc, g, t, weights, moving):
+            rows = slice(ROWS * g, ROWS * (g + 1))
+            w_cols = slice(P * t, P * (t + 1))
+            for c in range(HALF // MM_N):
+                cols = slice(MM_N * c, MM_N * (c + 1))
+                nc.tensor.matmul_mx(
+                    out=acc[:, cols],
+                    lhsT=weights[0][rows, w_cols].bitcast(FP8X4),
+                    lhsT_scale=weights[1][rows, w_cols],
+                    rhs=moving[0][rows, cols].bitcast(FP8X4),
+                    rhs_scale=moving[1][rows, cols],
+                    start=True,
+                    stop=True,
+                )
+
+        halves = [slice(HALF * h, HALF * (h + 1)) for h in range(HALVES)]
+        gt = [(g, t) for g in range(G) for t in range(TILES)]
+        hg = [(h, g) for h in range(HALVES) for g in range(G)]
+
+        w1_raw = load_rows("w1", packed_rows(w1))
+        x_raw = [load_rows("x%d" % h, packed_rows(x)[:, :, halves[h]]) for h in range(HALVES)]
+        w2_raw = load_rows("w2", packed_rows(w2))
+        wo2_raw = load_rows("wo2", packed_rows(wo2))
+        re_sb = load_per_feature("re", reserve)
+        hs_sb = load_per_feature("hs", hs)
+        ob_sb = load_per_feature("ob", ob)
+        osc_sb = load_per_feature("osc", osc)
+
+        bank_a = {(g, i): ps.tile([P, N], F32, name="bank_a%d%d" % (g, i)) for g, i in gt}
+        bank_b = {(g, i): ps.tile([P, N], F32, name="bank_b%d%d" % (g, i)) for g, i in gt}
+
+        w1_q = quantize("w1", group_weights("w1", w1_raw), K)
+
+        x_q = []
+        expz = {(g, t): sb.tile([P, N], F32, name="expz%d%d" % (g, t)) for g, t in gt}
+        for h in range(HALVES):
+            grouped = sb.tile([P, HALF * PACK], BF16, name="x%d_grouped" % h, align_bytes=64)
+            dst = grouped[:].rearrange("p (n j) -> p n j", j=PACK)
+            src = x_raw[h][:].rearrange("p j n -> p n j")
+            if h == 0:
+                nc.vector.tensor_copy(out=dst[:, 0:160, :], in_=src[:, 0:160, :])
+                nc.scalar.copy(out=dst[:, 160:HALF, :], in_=src[:, 160:HALF, :])
+            else:
+                nc.vector.tensor_copy(out=dst, in_=src)
+            x_q.append(quantize("x%d" % h, grouped, HALF))
+            for g, t in gt:
+                multiply(bank_a[g, t][:, halves[h]], g, t, w1_q, x_q[h])
+            for g, t in gt:
+                nc.scalar.activation(out=expz[g, t][:, halves[h]], in_=bank_a[g, t][:, halves[h]], func=ACT.Exp)
+
+        w2_grouped = group_weights("w2", w2_raw)
+        capped = {(g, t): sb.tile([P, N], F32, name="capped%d%d" % (g, t)) for g, t in gt}
+        for i, (g, t) in enumerate(gt):
+            nc.vector.tensor_scalar_min(out=capped[g, t][:], in0=expz[g, t][:], scalar1=EXP_CAP)
+            if i == 0:
+                w2_q = quantize("w2", w2_grouped, K)
+        for h, g in hg:
+            for t in range(TILES):
+                multiply(bank_b[g, h][:, halves[t]], g, t, w2_q, x_q[h])
+        wo2_q = quantize("wo2", group_weights("wo2", wo2_raw), K)
+
+        logs = {(g, t): sb.tile([P, N], F32, name="logs%d%d" % (g, t)) for g, t in gt}
+        for g, t in gt:
+            nc.scalar.activation(out=logs[g, t][:], in_=capped[g, t][:], func=ACT.Ln, bias=1.0)
+
+        p1 = {(g, t): sb.tile([P, N], F32, name="p1_%d%d" % (g, t)) for g, t in gt}
+        sums = [sb.tile([P, TILES], F32, name="sums%d" % g) for g in range(G)]
+        zs = [sb.tile([P, TILES], F32, name="zs%d" % g) for g in range(G)]
+        inv = [sb.tile([P, TILES], F32, name="inv%d" % g) for g in range(G)]
+        share = [sb.tile([P, TILES, N], F32, name="share%d" % g) for g in range(G)]
+
+        def softplus(g, t):
+            nc.vector.scalar_tensor_tensor(
+                out=p1[g, t][:], in0=bank_a[g, t][:], scalar=1.0, in1=logs[g, t][:],
+                op0=ALU.mult, op1=ALU.max, accum_out=sums[g][:, t : t + 1],
+            )
+
+        def add_reserve(g):
+            nc.vector.tensor_tensor(out=zs[g][:], in0=sums[g][:], in1=re_sb[:, g, 0:TILES], op=ALU.add)
+
+        def invert(g):
+            nc.vector.reciprocal(out=inv[g][:], in_=zs[g][:])
+
+        def normalise(g, t):
+            nc.vector.tensor_scalar(
+                out=share[g][:, t, :], in0=p1[g, t][:], scalar1=inv[g][:, t : t + 1],
+                scalar2=hs_sb[:, g, t : t + 1], op0=ALU.mult, op1=ALU.mult,
+            )
+
+        gate = {}
+        for h, g in hg:
+            gate[h, g] = sb.tile([P, HALF, TILES], F32, name="gate%d%d" % (h, g))
+            nc.scalar.activation(
+                out=gate[h, g][:], in_=bank_b[g, h][:].rearrange("p (t n) -> p n t", t=TILES), func=ACT.Tanh
+            )
+
+        gathered = [sb.tile([P, 2, HALF * TILES], BF16, name="gathered%d" % h, align_bytes=64) for h in range(HALVES)]
+
+        def gated(h, g):
+            pairs = sb.tile([P, HALF * TILES], BF16, name="pairs%d%d" % (h, g), align_bytes=64)
+            nc.vector.scalar_tensor_tensor(
+                out=pairs[:].rearrange("p (n t) -> p n t", t=TILES),
+                in0=share[g][:, :, halves[h]].rearrange("p t n -> p n t"), scalar=float(N),
+                in1=gate[h, g][:], op0=ALU.mult, op1=ALU.mult,
+            )
+            nc.sync.dma_start(out=gathered[h][ROWS * g : ROWS * (g + 1), :, :], in_=pairs[:])
+
+        softplus(0, 0)
+        softplus(0, 1)
+        softplus(1, 0)
+        add_reserve(0)
+        softplus(1, 1)
+        invert(0)
+        add_reserve(1)
+        normalise(0, 0)
+        invert(1)
+        normalise(0, 1)
+        normalise(1, 0)
+        gated(0, 0)
+        normalise(1, 1)
+        gated(0, 1)
+        gated(1, 0)
+        gated(1, 1)
+
+        def second_product(h):
+            grouped = sb.tile([P, HALF * PACK], BF16, name="hh%d_grouped" % h, align_bytes=64)
+            nc.vector.tensor_copy(
+                out=grouped[:].bitcast(F32).rearrange("p (n u) -> p n u", u=2),
+                in_=gathered[h][:].bitcast(F32).rearrange("p u n -> p n u"),
+            )
+            hh_q = quantize("hh%d" % h, grouped, HALF)
+            for g, t in gt:
+                multiply(bank_a[g, h][:, halves[t]], g, t, wo2_q, hh_q)
+
+        def finish(h, g):
+            act = sb.tile([P, TILES, HALF], F32, name="act%d%d" % (h, g))
+            res = sb.tile([P, TILES, HALF], F32, name="res%d%d" % (h, g))
+            for t in range(TILES):
+                nc.scalar.activation(
+                    out=act[:, t, :], in_=bank_a[g, h][:, halves[t]], func=ACT.Tanh, bias=ob_sb[:, g, t : t + 1]
+                )
+                nc.vector.tensor_scalar_mul(out=res[:, t, :], in0=act[:, t, :], scalar1=osc_sb[:, g, t : t + 1])
+            nc.sync.dma_start(out=out[g].rearrange("(q t) n -> q t n", t=TILES)[:, :, halves[h]], in_=res[:])
+
+        for h in range(HALVES):
+            second_product(h)
+        for h, g in hg:
+            finish(h, g)

@@ -1,3 +1,4 @@
+import math
 from contextlib import ExitStack
 
 import concourse.mybir as mybir
@@ -19,7 +20,8 @@ TILES = K // P
 HALVES = 2
 HALF = N // HALVES
 MM_N = 128
-EXP_CAP = 2.0**60
+CHUNKS = N // MM_N
+KNEE = 32.0
 
 FLOPS = 3 * 2 * G * K * K * N
 
@@ -51,18 +53,24 @@ def tile_rows_frowshare_kernel(tc, x, w1, w2, reserve, hs, wo2, ob, osc, out):
             nc.vector.quantize_mx(out=codes[:].bitcast(FP8X4), scales=scales[:], in_=grouped[:])
             return codes, scales
 
-        def group_weights(name, raw):
+        def interleave(dst, src, on_vector):
+            nc.vector.tensor_copy(out=dst[:, 0:on_vector], in_=src[:, 0:on_vector])
+            if on_vector < dst.shape[1]:
+                nc.scalar.copy(out=dst[:, on_vector:], in_=src[:, on_vector:])
+
+        def group_weights(name, raw, on_vector):
             grouped = sb.tile([P, K * PACK], BF16, name=name + "_grouped", align_bytes=64)
-            nc.vector.tensor_copy(
-                out=grouped[:].rearrange("p (t q j) -> p t q j", t=TILES, j=PACK),
-                in_=raw[:].rearrange("p j (q t) -> p t q j", t=TILES),
+            interleave(
+                grouped[:].rearrange("p (t c r j) -> p c j r t", t=TILES, r=2, j=PACK),
+                raw[:].rearrange("p j (c r t) -> p c j r t", r=2, t=TILES),
+                on_vector,
             )
             return grouped
 
-        def multiply(acc, g, t, weights, moving):
+        def multiply(acc, g, t, weights, moving, width):
             rows = slice(ROWS * g, ROWS * (g + 1))
             w_cols = slice(P * t, P * (t + 1))
-            for c in range(HALF // MM_N):
+            for c in range(width // MM_N):
                 cols = slice(MM_N * c, MM_N * (c + 1))
                 nc.tensor.matmul_mx(
                     out=acc[:, cols],
@@ -90,120 +98,156 @@ def tile_rows_frowshare_kernel(tc, x, w1, w2, reserve, hs, wo2, ob, osc, out):
         bank_a = {(g, i): ps.tile([P, N], F32, name="bank_a%d%d" % (g, i)) for g, i in gt}
         bank_b = {(g, i): ps.tile([P, N], F32, name="bank_b%d%d" % (g, i)) for g, i in gt}
 
-        w1_q = quantize("w1", group_weights("w1", w1_raw), K)
+        w1_q = quantize("w1", group_weights("w1", w1_raw, 42), K)
 
         x_q = []
         expz = {(g, t): sb.tile([P, N], F32, name="expz%d%d" % (g, t)) for g, t in gt}
         for h in range(HALVES):
             grouped = sb.tile([P, HALF * PACK], BF16, name="x%d_grouped" % h, align_bytes=64)
-            dst = grouped[:].rearrange("p (n j) -> p n j", j=PACK)
-            src = x_raw[h][:].rearrange("p j n -> p n j")
-            if h == 0:
-                nc.vector.tensor_copy(out=dst[:, 0:160, :], in_=src[:, 0:160, :])
-                nc.scalar.copy(out=dst[:, 160:HALF, :], in_=src[:, 160:HALF, :])
-            else:
-                nc.vector.tensor_copy(out=dst, in_=src)
+            interleave(
+                grouped[:].rearrange("p (c i j) -> p c j i", i=4, j=PACK),
+                x_raw[h][:].rearrange("p j (c i) -> p c j i", i=4),
+                42 if h == 0 else 64,
+            )
             x_q.append(quantize("x%d" % h, grouped, HALF))
             for g, t in gt:
-                multiply(bank_a[g, t][:, halves[h]], g, t, w1_q, x_q[h])
+                multiply(bank_a[g, t][:, halves[h]], g, t, w1_q, x_q[h], HALF)
             for g, t in gt:
                 nc.scalar.activation(out=expz[g, t][:, halves[h]], in_=bank_a[g, t][:, halves[h]], func=ACT.Exp)
 
-        w2_grouped = group_weights("w2", w2_raw)
-        capped = {(g, t): sb.tile([P, N], F32, name="capped%d%d" % (g, t)) for g, t in gt}
-        for i, (g, t) in enumerate(gt):
-            nc.vector.tensor_scalar_min(out=capped[g, t][:], in0=expz[g, t][:], scalar1=EXP_CAP)
-            if i == 0:
-                w2_q = quantize("w2", w2_grouped, K)
+        w2_q = quantize("w2", group_weights("w2", w2_raw, 64), K)
         for h, g in hg:
             for t in range(TILES):
-                multiply(bank_b[g, h][:, halves[t]], g, t, w2_q, x_q[h])
-        wo2_q = quantize("wo2", group_weights("wo2", wo2_raw), K)
+                multiply(bank_b[g, h][:, halves[t]], g, t, w2_q, x_q[h], HALF)
 
+        capped = {(g, t): sb.tile([P, N], F32, name="capped%d%d" % (g, t)) for g, t in gt}
+        stretch = {(g, t): sb.tile([P, N], F32, name="stretch%d%d" % (g, t)) for g, t in gt}
         logs = {(g, t): sb.tile([P, N], F32, name="logs%d%d" % (g, t)) for g, t in gt}
-        for g, t in gt:
-            nc.scalar.activation(out=logs[g, t][:], in_=capped[g, t][:], func=ACT.Ln, bias=1.0)
-
-        p1 = {(g, t): sb.tile([P, N], F32, name="p1_%d%d" % (g, t)) for g, t in gt}
+        excess = [sb.tile([P, TILES], F32, name="excess%d" % g) for g in range(G)]
+        base = [sb.tile([P, TILES], F32, name="base%d" % g) for g in range(G)]
         sums = [sb.tile([P, TILES], F32, name="sums%d" % g) for g in range(G)]
         zs = [sb.tile([P, TILES], F32, name="zs%d" % g) for g in range(G)]
         inv = [sb.tile([P, TILES], F32, name="inv%d" % g) for g in range(G)]
+        factor = [sb.tile([P, TILES], F32, name="factor%d" % g) for g in range(G)]
         share = [sb.tile([P, TILES, N], F32, name="share%d" % g) for g in range(G)]
 
-        def softplus(g, t):
-            nc.vector.scalar_tensor_tensor(
-                out=p1[g, t][:], in0=bank_a[g, t][:], scalar=1.0, in1=logs[g, t][:],
-                op0=ALU.mult, op1=ALU.max, accum_out=sums[g][:, t : t + 1],
+        def cap(g, t):
+            nc.gpsimd.tensor_scalar(
+                out=capped[g, t][:], in0=expz[g, t][:], scalar1=math.exp(KNEE), scalar2=0.0,
+                op0=ALU.min, op1=ALU.max,
+            )
+
+        def beyond_knee(g, t):
+            nc.vector.tensor_scalar(
+                out=stretch[g, t][:], in0=bank_a[g, t][:], scalar1=KNEE, scalar2=-N * KNEE,
+                op0=ALU.max, op1=ALU.add, accum_out=excess[g][:, t : t + 1],
             )
 
         def add_reserve(g):
-            nc.vector.tensor_tensor(out=zs[g][:], in0=sums[g][:], in1=re_sb[:, g, 0:TILES], op=ALU.add)
+            nc.vector.tensor_tensor(out=base[g][:], in0=excess[g][:], in1=re_sb[:, g, 0:TILES], op=ALU.add)
+
+        def total(g):
+            nc.vector.tensor_tensor(out=zs[g][:], in0=sums[g][:], in1=base[g][:], op=ALU.add)
+
+        def weigh(g):
+            nc.vector.tensor_tensor(out=factor[g][:], in0=inv[g][:], in1=hs_sb[:, g, 0:TILES], op=ALU.mult)
+
+        for g, t in gt:
+            beyond_knee(g, t)
+            cap(g, t)
+            if t == TILES - 1:
+                add_reserve(g)
+        for g, t in gt:
+            nc.scalar.activation(
+                out=logs[g, t][:], in_=capped[g, t][:], func=ACT.Ln, bias=1.0, accum_out=sums[g][:, t : t + 1]
+            )
 
         def invert(g):
             nc.vector.reciprocal(out=inv[g][:], in_=zs[g][:])
 
         def normalise(g, t):
-            nc.vector.tensor_scalar(
-                out=share[g][:, t, :], in0=p1[g, t][:], scalar1=inv[g][:, t : t + 1],
-                scalar2=hs_sb[:, g, t : t + 1], op0=ALU.mult, op1=ALU.mult,
+            nc.vector.scalar_tensor_tensor(
+                out=share[g][:, t, :], in0=logs[g, t][:], scalar=factor[g][:, t : t + 1],
+                in1=stretch[g, t][:], op0=ALU.mult, op1=ALU.mult,
             )
 
+        chunks = [slice(MM_N * c, MM_N * (c + 1)) for c in range(CHUNKS)]
+        cg = [(c, g) for c in range(CHUNKS) for g in range(G)]
         gate = {}
-        for h, g in hg:
-            gate[h, g] = sb.tile([P, HALF, TILES], F32, name="gate%d%d" % (h, g))
+        for c, g in cg:
+            gate[c, g] = sb.tile([P, MM_N, TILES], F32, name="gate%d%d" % (c, g))
             nc.scalar.activation(
-                out=gate[h, g][:], in_=bank_b[g, h][:].rearrange("p (t n) -> p n t", t=TILES), func=ACT.Tanh
+                out=gate[c, g][:],
+                in_=bank_b[g, c // 2][:].rearrange("p (t n) -> p n t", t=TILES)[:, chunks[c % 2], :],
+                func=ACT.Tanh,
             )
 
-        gathered = [sb.tile([P, 2, HALF * TILES], BF16, name="gathered%d" % h, align_bytes=64) for h in range(HALVES)]
+        gathered = [sb.tile([P, 2, MM_N * TILES], BF16, name="gathered%d" % c, align_bytes=64) for c in range(CHUNKS)]
 
-        def gated(h, g):
-            pairs = sb.tile([P, HALF * TILES], BF16, name="pairs%d%d" % (h, g), align_bytes=64)
+        def gated(c, g):
+            pairs = sb.tile([P, MM_N * TILES], BF16, name="pairs%d%d" % (c, g), align_bytes=64)
             nc.vector.scalar_tensor_tensor(
                 out=pairs[:].rearrange("p (n t) -> p n t", t=TILES),
-                in0=share[g][:, :, halves[h]].rearrange("p t n -> p n t"), scalar=float(N),
-                in1=gate[h, g][:], op0=ALU.mult, op1=ALU.mult,
+                in0=share[g][:, :, chunks[c]].rearrange("p t n -> p n t"), scalar=N / KNEE,
+                in1=gate[c, g][:], op0=ALU.mult, op1=ALU.mult,
             )
-            nc.sync.dma_start(out=gathered[h][ROWS * g : ROWS * (g + 1), :, :], in_=pairs[:])
+            nc.sync.dma_start(out=gathered[c][ROWS * g : ROWS * (g + 1), :, :], in_=pairs[:])
 
-        softplus(0, 0)
-        softplus(0, 1)
-        softplus(1, 0)
-        add_reserve(0)
-        softplus(1, 1)
+        wo2_grouped = group_weights("wo2", wo2_raw, 64)
+        total(0)
         invert(0)
-        add_reserve(1)
+        weigh(0)
         normalise(0, 0)
-        invert(1)
+        total(1)
         normalise(0, 1)
+        invert(1)
+        weigh(1)
         normalise(1, 0)
-        gated(0, 0)
         normalise(1, 1)
-        gated(0, 1)
-        gated(1, 0)
-        gated(1, 1)
+        for c, g in cg:
+            gated(c, g)
+        wo2_q = quantize("wo2", wo2_grouped, K)
 
-        def second_product(h):
-            grouped = sb.tile([P, HALF * PACK], BF16, name="hh%d_grouped" % h, align_bytes=64)
+        y_bank = {(c, g): [bank_a, bank_b][c // 2][g, c % 2] for c, g in cg}
+        hh_grouped = {}
+
+        def pack_words(c):
+            hh_grouped[c] = sb.tile([P, MM_N * PACK], BF16, name="hh%d_grouped" % c, align_bytes=64)
             nc.vector.tensor_copy(
-                out=grouped[:].bitcast(F32).rearrange("p (n u) -> p n u", u=2),
-                in_=gathered[h][:].bitcast(F32).rearrange("p u n -> p n u"),
+                out=hh_grouped[c][:].bitcast(F32).rearrange("p (n u) -> p n u", u=2),
+                in_=gathered[c][:].bitcast(F32).rearrange("p u n -> p n u"),
             )
-            hh_q = quantize("hh%d" % h, grouped, HALF)
+
+        def second_product(c):
+            hh_q = quantize("hh%d" % c, hh_grouped[c], MM_N)
             for g, t in gt:
-                multiply(bank_a[g, h][:, halves[t]], g, t, wo2_q, hh_q)
+                multiply(y_bank[c, g][:, chunks[t]], g, t, wo2_q, hh_q, MM_N)
 
-        def finish(h, g):
-            act = sb.tile([P, TILES, HALF], F32, name="act%d%d" % (h, g))
-            res = sb.tile([P, TILES, HALF], F32, name="res%d%d" % (h, g))
-            for t in range(TILES):
-                nc.scalar.activation(
-                    out=act[:, t, :], in_=bank_a[g, h][:, halves[t]], func=ACT.Tanh, bias=ob_sb[:, g, t : t + 1]
-                )
-                nc.vector.tensor_scalar_mul(out=res[:, t, :], in0=act[:, t, :], scalar1=osc_sb[:, g, t : t + 1])
-            nc.sync.dma_start(out=out[g].rearrange("(q t) n -> q t n", t=TILES)[:, :, halves[h]], in_=res[:])
+        act = {}
 
-        for h in range(HALVES):
-            second_product(h)
-        for h, g in hg:
-            finish(h, g)
+        def activate(c):
+            for g in range(G):
+                act[c, g] = sb.tile([P, TILES, MM_N], F32, name="act%d%d" % (c, g))
+                for t in range(TILES):
+                    nc.scalar.activation(
+                        out=act[c, g][:, t, :], in_=y_bank[c, g][:, chunks[t]], func=ACT.Tanh,
+                        bias=ob_sb[:, g, t : t + 1],
+                    )
+
+        def finish(c):
+            for g in range(G):
+                res = sb.tile([P, TILES, MM_N], F32, name="res%d%d" % (c, g))
+                for t in range(TILES):
+                    nc.vector.tensor_scalar_mul(
+                        out=res[:, t, :], in0=act[c, g][:, t, :], scalar1=osc_sb[:, g, t : t + 1]
+                    )
+                nc.sync.dma_start(out=out[g].rearrange("(q t) n -> q t n", t=TILES)[:, :, chunks[c]], in_=res[:])
+
+        for c in range(CHUNKS + 2):
+            if c < CHUNKS:
+                pack_words(c)
+            if c >= 2:
+                finish(c - 2)
+            if c < CHUNKS:
+                second_product(c)
+                activate(c)

@@ -54,7 +54,8 @@ def tile_rows_frowshare_kernel(tc, x, w1, w2, reserve, hs, wo2, ob, osc, out):
             return codes, scales
 
         def interleave(dst, src, on_vector):
-            nc.vector.tensor_copy(out=dst[:, 0:on_vector], in_=src[:, 0:on_vector])
+            if on_vector > 0:
+                nc.vector.tensor_copy(out=dst[:, 0:on_vector], in_=src[:, 0:on_vector])
             if on_vector < dst.shape[1]:
                 nc.scalar.copy(out=dst[:, on_vector:], in_=src[:, on_vector:])
 
@@ -125,10 +126,10 @@ def tile_rows_frowshare_kernel(tc, x, w1, w2, reserve, hs, wo2, ob, osc, out):
         logs = {(g, t): sb.tile([P, N], F32, name="logs%d%d" % (g, t)) for g, t in gt}
         excess = [sb.tile([P, TILES], F32, name="excess%d" % g) for g in range(G)]
         base = [sb.tile([P, TILES], F32, name="base%d" % g) for g in range(G)]
-        sums = [sb.tile([P, TILES], F32, name="sums%d" % g) for g in range(G)]
-        zs = [sb.tile([P, TILES], F32, name="zs%d" % g) for g in range(G)]
-        inv = [sb.tile([P, TILES], F32, name="inv%d" % g) for g in range(G)]
-        factor = [sb.tile([P, TILES], F32, name="factor%d" % g) for g in range(G)]
+        sums = {(g, t): sb.tile([P, 1], F32, name="sums%d%d" % (g, t)) for g, t in gt}
+        zs = {(g, t): sb.tile([P, 1], F32, name="zs%d%d" % (g, t)) for g, t in gt}
+        factor = {(g, t): sb.tile([P, 1], F32, name="factor%d%d" % (g, t)) for g, t in gt}
+        hs_inv = sb.tile([P, G, TILES], F32, name="hs_inv")
         share = [sb.tile([P, TILES, N], F32, name="share%d" % g) for g in range(G)]
 
         def cap(g, t):
@@ -146,28 +147,29 @@ def tile_rows_frowshare_kernel(tc, x, w1, w2, reserve, hs, wo2, ob, osc, out):
         def add_reserve(g):
             nc.vector.tensor_tensor(out=base[g][:], in0=excess[g][:], in1=re_sb[:, g, 0:TILES], op=ALU.add)
 
-        def total(g):
-            nc.vector.tensor_tensor(out=zs[g][:], in0=sums[g][:], in1=base[g][:], op=ALU.add)
-
-        def weigh(g):
-            nc.vector.tensor_tensor(out=factor[g][:], in0=inv[g][:], in1=hs_sb[:, g, 0:TILES], op=ALU.mult)
+        def total(g, t):
+            nc.vector.tensor_scalar(
+                out=zs[g, t][:], in0=sums[g, t][:], scalar1=base[g][:, t : t + 1],
+                scalar2=hs_inv[:, g, t : t + 1], op0=ALU.add, op1=ALU.mult,
+            )
 
         for g, t in gt:
             beyond_knee(g, t)
             cap(g, t)
-            if t == TILES - 1:
-                add_reserve(g)
+        nc.vector.reciprocal(out=hs_inv[:], in_=hs_sb[:, :, 0:TILES])
+        for g in range(G):
+            add_reserve(g)
         for g, t in gt:
             nc.scalar.activation(
-                out=logs[g, t][:], in_=capped[g, t][:], func=ACT.Ln, bias=1.0, accum_out=sums[g][:, t : t + 1]
+                out=logs[g, t][:], in_=capped[g, t][:], func=ACT.Ln, bias=1.0, accum_out=sums[g, t][:]
             )
 
-        def invert(g):
-            nc.vector.reciprocal(out=inv[g][:], in_=zs[g][:])
+        def invert(g, t):
+            nc.vector.reciprocal(out=factor[g, t][:], in_=zs[g, t][:])
 
         def normalise(g, t):
             nc.vector.scalar_tensor_tensor(
-                out=share[g][:, t, :], in0=logs[g, t][:], scalar=factor[g][:, t : t + 1],
+                out=share[g][:, t, :], in0=logs[g, t][:], scalar=factor[g, t][:],
                 in1=stretch[g, t][:], op0=ALU.mult, op1=ALU.mult,
             )
 
@@ -193,17 +195,15 @@ def tile_rows_frowshare_kernel(tc, x, w1, w2, reserve, hs, wo2, ob, osc, out):
             )
             nc.sync.dma_start(out=gathered[c][ROWS * g : ROWS * (g + 1), :, :], in_=pairs[:])
 
-        wo2_grouped = group_weights("wo2", wo2_raw, 64)
-        total(0)
-        invert(0)
-        weigh(0)
-        normalise(0, 0)
-        total(1)
-        normalise(0, 1)
-        invert(1)
-        weigh(1)
-        normalise(1, 0)
-        normalise(1, 1)
+        wo2_grouped = group_weights("wo2", wo2_raw, 0)
+        total(*gt[0])
+        invert(*gt[0])
+        for i, (g, t) in enumerate(gt):
+            if i + 1 < len(gt):
+                total(*gt[i + 1])
+            normalise(g, t)
+            if i + 1 < len(gt):
+                invert(*gt[i + 1])
         for c, g in cg:
             gated(c, g)
         wo2_q = quantize("wo2", wo2_grouped, K)
@@ -246,8 +246,7 @@ def tile_rows_frowshare_kernel(tc, x, w1, w2, reserve, hs, wo2, ob, osc, out):
         for c in range(CHUNKS + 2):
             if c < CHUNKS:
                 pack_words(c)
-            if c >= 2:
-                finish(c - 2)
-            if c < CHUNKS:
                 second_product(c)
                 activate(c)
+            if c >= 2:
+                finish(c - 2)

@@ -33,6 +33,7 @@ def tile_rows_frowshare_kernel(tc, x, w1, w2, reserve, hs, wo2, ob, osc, out):
         sb = ctx.enter_context(tc.tile_pool(name="sb", bufs=1))
         ps = ctx.enter_context(tc.psum_pool(name="ps", bufs=1))
         ctx.enter_context(tc.manual_schedule())
+        ctx.enter_context(nc.allow_non_contiguous_dma(reason="one value a partition"))
 
         def load_rows(name, src):
             raw = sb.tile([P, PACK, src.shape[2]], F32, name=name + "_raw", align_bytes=64)
@@ -42,6 +43,11 @@ def tile_rows_frowshare_kernel(tc, x, w1, w2, reserve, hs, wo2, ob, osc, out):
         def load_per_feature(name, src):
             vec = sb.tile([P, G, 8], F32, name=name + "_sb")
             nc.sync.dma_start(out=vec[:, :, 0:TILES], in_=src.rearrange("g (q t) o -> q g (t o)", t=TILES))
+            return vec
+
+        def load_per_output(name, src):
+            vec = sb.tile([P, G * TILES, 8], F32, name=name + "_sb")
+            nc.sync.dma_start(out=vec[:, :, 0:1], in_=src.rearrange("g (t q) o -> q (g t) o", t=TILES))
             return vec
 
         def packed_rows(src):
@@ -54,8 +60,7 @@ def tile_rows_frowshare_kernel(tc, x, w1, w2, reserve, hs, wo2, ob, osc, out):
             return codes, scales
 
         def interleave(dst, src, on_vector):
-            if on_vector > 0:
-                nc.vector.tensor_copy(out=dst[:, 0:on_vector], in_=src[:, 0:on_vector])
+            nc.vector.tensor_copy(out=dst[:, 0:on_vector], in_=src[:, 0:on_vector])
             if on_vector < dst.shape[1]:
                 nc.scalar.copy(out=dst[:, on_vector:], in_=src[:, on_vector:])
 
@@ -93,8 +98,8 @@ def tile_rows_frowshare_kernel(tc, x, w1, w2, reserve, hs, wo2, ob, osc, out):
         wo2_raw = load_rows("wo2", packed_rows(wo2))
         re_sb = load_per_feature("re", reserve)
         hs_sb = load_per_feature("hs", hs)
-        ob_sb = load_per_feature("ob", ob)
-        osc_sb = load_per_feature("osc", osc)
+        ob_sb = load_per_output("ob", ob)
+        osc_sb = load_per_output("osc", osc)
 
         bank_a = {(g, i): ps.tile([P, N], F32, name="bank_a%d%d" % (g, i)) for g, i in gt}
         bank_b = {(g, i): ps.tile([P, N], F32, name="bank_b%d%d" % (g, i)) for g, i in gt}
@@ -156,6 +161,15 @@ def tile_rows_frowshare_kernel(tc, x, w1, w2, reserve, hs, wo2, ob, osc, out):
         for g, t in gt:
             beyond_knee(g, t)
             cap(g, t)
+        wo2_grouped = sb.tile([P, K * PACK], BF16, name="wo2_grouped", align_bytes=64)
+        wo2_dst = wo2_grouped[:].rearrange("p (c i j) -> p c j i", i=4, j=PACK)
+        wo2_src = wo2_raw[:].rearrange("p j (c i) -> p c j i", i=4)
+        nc.vector.tensor_copy(out=wo2_dst[:, 0:32], in_=wo2_src[:, 0:32])
+        nc.gpsimd.tensor_scalar(
+            out=wo2_grouped[:].rearrange("p (n j) -> p n j", j=PACK)[:, P:, :],
+            in0=wo2_raw[:].rearrange("p j n -> p n j")[:, P:, :],
+            scalar1=1.0, scalar2=0.0, op0=ALU.mult, op1=ALU.add,
+        )
         nc.vector.reciprocal(out=hs_inv[:], in_=hs_sb[:, :, 0:TILES])
         for g in range(G):
             add_reserve(g)
@@ -195,7 +209,6 @@ def tile_rows_frowshare_kernel(tc, x, w1, w2, reserve, hs, wo2, ob, osc, out):
             )
             nc.sync.dma_start(out=gathered[c][ROWS * g : ROWS * (g + 1), :, :], in_=pairs[:])
 
-        wo2_grouped = group_weights("wo2", wo2_raw, 0)
         total(*gt[0])
         invert(*gt[0])
         for i, (g, t) in enumerate(gt):
@@ -204,9 +217,9 @@ def tile_rows_frowshare_kernel(tc, x, w1, w2, reserve, hs, wo2, ob, osc, out):
             normalise(g, t)
             if i + 1 < len(gt):
                 invert(*gt[i + 1])
+        wo2_q = quantize("wo2", wo2_grouped, K)
         for c, g in cg:
             gated(c, g)
-        wo2_q = quantize("wo2", wo2_grouped, K)
 
         y_bank = {(c, g): [bank_a, bank_b][c // 2][g, c % 2] for c, g in cg}
         hh_grouped = {}
@@ -231,7 +244,7 @@ def tile_rows_frowshare_kernel(tc, x, w1, w2, reserve, hs, wo2, ob, osc, out):
                 for t in range(TILES):
                     nc.scalar.activation(
                         out=act[c, g][:, t, :], in_=y_bank[c, g][:, chunks[t]], func=ACT.Tanh,
-                        bias=ob_sb[:, g, t : t + 1],
+                        bias=ob_sb[:, TILES * g + t, 0:1],
                     )
 
         def finish(c):
@@ -239,9 +252,9 @@ def tile_rows_frowshare_kernel(tc, x, w1, w2, reserve, hs, wo2, ob, osc, out):
                 res = sb.tile([P, TILES, MM_N], F32, name="res%d%d" % (c, g))
                 for t in range(TILES):
                     nc.vector.tensor_scalar_mul(
-                        out=res[:, t, :], in0=act[c, g][:, t, :], scalar1=osc_sb[:, g, t : t + 1]
+                        out=res[:, t, :], in0=act[c, g][:, t, :], scalar1=osc_sb[:, TILES * g + t, 0:1]
                     )
-                nc.sync.dma_start(out=out[g].rearrange("(q t) n -> q t n", t=TILES)[:, :, chunks[c]], in_=res[:])
+                nc.sync.dma_start(out=out[g].rearrange("(t q) n -> q t n", t=TILES)[:, :, chunks[c]], in_=res[:])
 
         for c in range(CHUNKS + 2):
             if c < CHUNKS:

@@ -5,14 +5,15 @@ import concourse.mybir as mybir
 
 F32 = mybir.dt.float32
 BF16 = mybir.dt.bfloat16
-I32 = mybir.dt.int32
 U32 = mybir.dt.uint32
 U8 = mybir.dt.uint8
 FP8X4 = mybir.dt.float8_e4m3fn_x4
 ACT = mybir.ActivationFunctionType
 ALU = mybir.AluOpType
 
-G, K, N = 2, 256, 512
+G = 2
+K = 256
+N = 512
 P = 128
 PACK = 4
 ROWS = K // PACK
@@ -21,6 +22,11 @@ HALVES = 2
 HALF = N // HALVES
 MM_N = 128
 CHUNKS = N // MM_N
+LINE = 4
+LINES = K // LINE
+VECTOR_LINES = 42
+FINISH_LAG = 2
+PAD = 8
 KNEE = 32.0
 
 FLOPS = 3 * 2 * G * K * K * N
@@ -33,7 +39,10 @@ def tile_rows_frowshare_kernel(tc, x, w1, w2, reserve, hs, wo2, ob, osc, out):
         sb = ctx.enter_context(tc.tile_pool(name="sb", bufs=1))
         ps = ctx.enter_context(tc.psum_pool(name="ps", bufs=1))
         ctx.enter_context(tc.manual_schedule())
-        ctx.enter_context(nc.allow_non_contiguous_dma(reason="one value a partition"))
+        ctx.enter_context(nc.allow_non_contiguous_dma(reason="ob and osc: one value a partition"))
+
+        def packed_rows(src):
+            return src.rearrange("g (p j) c -> (g p) j c", j=PACK)
 
         def load_rows(name, src):
             raw = sb.tile([P, PACK, src.shape[2]], F32, name=name + "_raw", align_bytes=64)
@@ -41,17 +50,14 @@ def tile_rows_frowshare_kernel(tc, x, w1, w2, reserve, hs, wo2, ob, osc, out):
             return raw
 
         def load_per_feature(name, src):
-            vec = sb.tile([P, G, 8], F32, name=name + "_sb")
+            vec = sb.tile([P, G, PAD], F32, name=name + "_sb")
             nc.sync.dma_start(out=vec[:, :, 0:TILES], in_=src.rearrange("g (q t) o -> q g (t o)", t=TILES))
             return vec
 
         def load_per_output(name, src):
-            vec = sb.tile([P, G * TILES, 8], F32, name=name + "_sb")
+            vec = sb.tile([P, G * TILES, PAD], F32, name=name + "_sb")
             nc.sync.dma_start(out=vec[:, :, 0:1], in_=src.rearrange("g (t q) o -> q (g t) o", t=TILES))
             return vec
-
-        def packed_rows(src):
-            return src.rearrange("g (p j) c -> (g p) j c", j=PACK)
 
         def quantize(name, grouped, width):
             codes = sb.tile([P, width], U32, name=name + "_codes", align_bytes=64)
@@ -59,25 +65,25 @@ def tile_rows_frowshare_kernel(tc, x, w1, w2, reserve, hs, wo2, ob, osc, out):
             nc.vector.quantize_mx(out=codes[:].bitcast(FP8X4), scales=scales[:], in_=grouped[:])
             return codes, scales
 
-        def interleave(dst, src, on_vector):
-            nc.vector.tensor_copy(out=dst[:, 0:on_vector], in_=src[:, 0:on_vector])
-            if on_vector < dst.shape[1]:
-                nc.scalar.copy(out=dst[:, on_vector:], in_=src[:, on_vector:])
+        def interleave(dst, src, vector_lines):
+            nc.vector.tensor_copy(out=dst[:, 0:vector_lines], in_=src[:, 0:vector_lines])
+            if vector_lines < LINES:
+                nc.scalar.copy(out=dst[:, vector_lines:], in_=src[:, vector_lines:])
 
-        def group_weights(name, raw, on_vector):
+        def deal_weights(name, raw, vector_lines):
             grouped = sb.tile([P, K * PACK], BF16, name=name + "_grouped", align_bytes=64)
             interleave(
-                grouped[:].rearrange("p (t c r j) -> p c j r t", t=TILES, r=2, j=PACK),
-                raw[:].rearrange("p j (c r t) -> p c j r t", r=2, t=TILES),
-                on_vector,
+                grouped[:].rearrange("p (t c r j) -> p c j r t", t=TILES, r=LINE // TILES, j=PACK),
+                raw[:].rearrange("p j (c r t) -> p c j r t", r=LINE // TILES, t=TILES),
+                vector_lines,
             )
             return grouped
 
         def multiply(acc, g, t, weights, moving, width):
             rows = slice(ROWS * g, ROWS * (g + 1))
             w_cols = slice(P * t, P * (t + 1))
-            for c in range(width // MM_N):
-                cols = slice(MM_N * c, MM_N * (c + 1))
+            for n0 in range(0, width, MM_N):
+                cols = slice(n0, n0 + MM_N)
                 nc.tensor.matmul_mx(
                     out=acc[:, cols],
                     lhsT=weights[0][rows, w_cols].bitcast(FP8X4),
@@ -89,42 +95,43 @@ def tile_rows_frowshare_kernel(tc, x, w1, w2, reserve, hs, wo2, ob, osc, out):
                 )
 
         halves = [slice(HALF * h, HALF * (h + 1)) for h in range(HALVES)]
+        chunks = [slice(MM_N * c, MM_N * (c + 1)) for c in range(CHUNKS)]
         gt = [(g, t) for g in range(G) for t in range(TILES)]
         hg = [(h, g) for h in range(HALVES) for g in range(G)]
+        cg = [(c, g) for c in range(CHUNKS) for g in range(G)]
 
         w1_raw = load_rows("w1", packed_rows(w1))
         x_raw = [load_rows("x%d" % h, packed_rows(x)[:, :, halves[h]]) for h in range(HALVES)]
         w2_raw = load_rows("w2", packed_rows(w2))
-        wo2_raw = load_rows("wo2", packed_rows(wo2))
         re_sb = load_per_feature("re", reserve)
         hs_sb = load_per_feature("hs", hs)
+        wo2_raw = load_rows("wo2", packed_rows(wo2))
         ob_sb = load_per_output("ob", ob)
         osc_sb = load_per_output("osc", osc)
 
         bank_a = {(g, i): ps.tile([P, N], F32, name="bank_a%d%d" % (g, i)) for g, i in gt}
         bank_b = {(g, i): ps.tile([P, N], F32, name="bank_b%d%d" % (g, i)) for g, i in gt}
 
-        w1_q = quantize("w1", group_weights("w1", w1_raw, 42), K)
-
+        w1_q = quantize("w1", deal_weights("w1", w1_raw, VECTOR_LINES), K)
         x_q = []
         expz = {(g, t): sb.tile([P, N], F32, name="expz%d%d" % (g, t)) for g, t in gt}
         for h in range(HALVES):
-            grouped = sb.tile([P, HALF * PACK], BF16, name="x%d_grouped" % h, align_bytes=64)
+            x_grouped = sb.tile([P, HALF * PACK], BF16, name="x%d_grouped" % h, align_bytes=64)
             interleave(
-                grouped[:].rearrange("p (c i j) -> p c j i", i=4, j=PACK),
-                x_raw[h][:].rearrange("p j (c i) -> p c j i", i=4),
-                42 if h == 0 else 64,
+                x_grouped[:].rearrange("p (c i j) -> p c j i", i=LINE, j=PACK),
+                x_raw[h][:].rearrange("p j (c i) -> p c j i", i=LINE),
+                VECTOR_LINES if h == 0 else LINES,
             )
-            x_q.append(quantize("x%d" % h, grouped, HALF))
+            x_q.append(quantize("x%d" % h, x_grouped, HALF))
             for g, t in gt:
                 multiply(bank_a[g, t][:, halves[h]], g, t, w1_q, x_q[h], HALF)
             for g, t in gt:
                 nc.scalar.activation(out=expz[g, t][:, halves[h]], in_=bank_a[g, t][:, halves[h]], func=ACT.Exp)
 
-        w2_q = quantize("w2", group_weights("w2", w2_raw, 64), K)
+        w2_q = quantize("w2", deal_weights("w2", w2_raw, LINES), K)
         for h, g in hg:
             for t in range(TILES):
-                multiply(bank_b[g, h][:, halves[t]], g, t, w2_q, x_q[h], HALF)
+                multiply(bank_b[g, h][:, HALF * t : HALF * (t + 1)], g, t, w2_q, x_q[h], HALF)
 
         capped = {(g, t): sb.tile([P, N], F32, name="capped%d%d" % (g, t)) for g, t in gt}
         stretch = {(g, t): sb.tile([P, N], F32, name="stretch%d%d" % (g, t)) for g, t in gt}
@@ -137,45 +144,48 @@ def tile_rows_frowshare_kernel(tc, x, w1, w2, reserve, hs, wo2, ob, osc, out):
         hs_inv = sb.tile([P, G, TILES], F32, name="hs_inv")
         share = [sb.tile([P, TILES, N], F32, name="share%d" % g) for g in range(G)]
 
-        def cap(g, t):
+        for g, t in gt:
+            nc.vector.tensor_scalar(
+                out=stretch[g, t][:], in0=bank_a[g, t][:], scalar1=KNEE, scalar2=-N * KNEE,
+                op0=ALU.max, op1=ALU.add, accum_out=excess[g][:, t : t + 1],
+            )
             nc.gpsimd.tensor_scalar(
                 out=capped[g, t][:], in0=expz[g, t][:], scalar1=math.exp(KNEE), scalar2=0.0,
                 op0=ALU.min, op1=ALU.max,
             )
 
-        def beyond_knee(g, t):
-            nc.vector.tensor_scalar(
-                out=stretch[g, t][:], in0=bank_a[g, t][:], scalar1=KNEE, scalar2=-N * KNEE,
-                op0=ALU.max, op1=ALU.add, accum_out=excess[g][:, t : t + 1],
-            )
-
-        def add_reserve(g):
+        wo2_grouped = sb.tile([P, K * PACK], BF16, name="wo2_grouped", align_bytes=64)
+        nc.vector.tensor_copy(
+            out=wo2_grouped[:].rearrange("p (c i j) -> p c j i", i=LINE, j=PACK)[:, 0 : P // LINE],
+            in_=wo2_raw[:].rearrange("p j (c i) -> p c j i", i=LINE)[:, 0 : P // LINE],
+        )
+        nc.gpsimd.tensor_scalar(
+            out=wo2_grouped[:].rearrange("p (o j) -> p o j", j=PACK)[:, P:, :],
+            in0=wo2_raw[:].rearrange("p j o -> p o j")[:, P:, :],
+            scalar1=1.0, scalar2=0.0, op0=ALU.mult, op1=ALU.add,
+        )
+        nc.vector.reciprocal(out=hs_inv[:], in_=hs_sb[:, :, 0:TILES])
+        for g in range(G):
             nc.vector.tensor_tensor(out=base[g][:], in0=excess[g][:], in1=re_sb[:, g, 0:TILES], op=ALU.add)
+
+        for g, t in gt:
+            nc.scalar.activation(
+                out=logs[g, t][:], in_=capped[g, t][:], func=ACT.Ln, bias=1.0, accum_out=sums[g, t][:]
+            )
+        gate = {}
+        for c, g in cg:
+            h, part = divmod(c, CHUNKS // HALVES)
+            gate[c, g] = sb.tile([P, MM_N, TILES], F32, name="gate%d%d" % (c, g))
+            nc.scalar.activation(
+                out=gate[c, g][:],
+                in_=bank_b[g, h][:].rearrange("p (t n) -> p n t", t=TILES)[:, chunks[part], :],
+                func=ACT.Tanh,
+            )
 
         def total(g, t):
             nc.vector.tensor_scalar(
                 out=zs[g, t][:], in0=sums[g, t][:], scalar1=base[g][:, t : t + 1],
                 scalar2=hs_inv[:, g, t : t + 1], op0=ALU.add, op1=ALU.mult,
-            )
-
-        for g, t in gt:
-            beyond_knee(g, t)
-            cap(g, t)
-        wo2_grouped = sb.tile([P, K * PACK], BF16, name="wo2_grouped", align_bytes=64)
-        wo2_dst = wo2_grouped[:].rearrange("p (c i j) -> p c j i", i=4, j=PACK)
-        wo2_src = wo2_raw[:].rearrange("p j (c i) -> p c j i", i=4)
-        nc.vector.tensor_copy(out=wo2_dst[:, 0:32], in_=wo2_src[:, 0:32])
-        nc.gpsimd.tensor_scalar(
-            out=wo2_grouped[:].rearrange("p (n j) -> p n j", j=PACK)[:, P:, :],
-            in0=wo2_raw[:].rearrange("p j n -> p n j")[:, P:, :],
-            scalar1=1.0, scalar2=0.0, op0=ALU.mult, op1=ALU.add,
-        )
-        nc.vector.reciprocal(out=hs_inv[:], in_=hs_sb[:, :, 0:TILES])
-        for g in range(G):
-            add_reserve(g)
-        for g, t in gt:
-            nc.scalar.activation(
-                out=logs[g, t][:], in_=capped[g, t][:], func=ACT.Ln, bias=1.0, accum_out=sums[g, t][:]
             )
 
         def invert(g, t):
@@ -187,20 +197,18 @@ def tile_rows_frowshare_kernel(tc, x, w1, w2, reserve, hs, wo2, ob, osc, out):
                 in1=stretch[g, t][:], op0=ALU.mult, op1=ALU.mult,
             )
 
-        chunks = [slice(MM_N * c, MM_N * (c + 1)) for c in range(CHUNKS)]
-        cg = [(c, g) for c in range(CHUNKS) for g in range(G)]
-        gate = {}
+        total(*gt[0])
+        invert(*gt[0])
+        for this, following in zip(gt, gt[1:]):
+            total(*following)
+            normalise(*this)
+            invert(*following)
+        normalise(*gt[-1])
+
+        gathered = [
+            sb.tile([P, P // ROWS, MM_N * TILES], BF16, name="gathered%d" % c, align_bytes=64) for c in range(CHUNKS)
+        ]
         for c, g in cg:
-            gate[c, g] = sb.tile([P, MM_N, TILES], F32, name="gate%d%d" % (c, g))
-            nc.scalar.activation(
-                out=gate[c, g][:],
-                in_=bank_b[g, c // 2][:].rearrange("p (t n) -> p n t", t=TILES)[:, chunks[c % 2], :],
-                func=ACT.Tanh,
-            )
-
-        gathered = [sb.tile([P, 2, MM_N * TILES], BF16, name="gathered%d" % c, align_bytes=64) for c in range(CHUNKS)]
-
-        def gated(c, g):
             pairs = sb.tile([P, MM_N * TILES], BF16, name="pairs%d%d" % (c, g), align_bytes=64)
             nc.vector.scalar_tensor_tensor(
                 out=pairs[:].rearrange("p (n t) -> p n t", t=TILES),
@@ -209,57 +217,46 @@ def tile_rows_frowshare_kernel(tc, x, w1, w2, reserve, hs, wo2, ob, osc, out):
             )
             nc.sync.dma_start(out=gathered[c][ROWS * g : ROWS * (g + 1), :, :], in_=pairs[:])
 
-        total(*gt[0])
-        invert(*gt[0])
-        for i, (g, t) in enumerate(gt):
-            if i + 1 < len(gt):
-                total(*gt[i + 1])
-            normalise(g, t)
-            if i + 1 < len(gt):
-                invert(*gt[i + 1])
-        wo2_q = quantize("wo2", wo2_grouped, K)
-        for c, g in cg:
-            gated(c, g)
-
-        y_bank = {(c, g): [bank_a, bank_b][c // 2][g, c % 2] for c, g in cg}
+        y_bank = {(c, g): [bank_a, bank_b][c // TILES][g, c % TILES] for c, g in cg}
+        y_cols = [slice(MM_N * t, MM_N * (t + 1)) for t in range(TILES)]
         hh_grouped = {}
+        act = {}
 
         def pack_words(c):
             hh_grouped[c] = sb.tile([P, MM_N * PACK], BF16, name="hh%d_grouped" % c, align_bytes=64)
             nc.vector.tensor_copy(
-                out=hh_grouped[c][:].bitcast(F32).rearrange("p (n u) -> p n u", u=2),
+                out=hh_grouped[c][:].bitcast(F32).rearrange("p (n u) -> p n u", u=P // ROWS),
                 in_=gathered[c][:].bitcast(F32).rearrange("p u n -> p n u"),
             )
 
-        def second_product(c):
+        def second_layer(c, wo2_q):
             hh_q = quantize("hh%d" % c, hh_grouped[c], MM_N)
             for g, t in gt:
-                multiply(y_bank[c, g][:, chunks[t]], g, t, wo2_q, hh_q, MM_N)
-
-        act = {}
-
-        def activate(c):
+                multiply(y_bank[c, g][:, y_cols[t]], g, t, wo2_q, hh_q, MM_N)
             for g in range(G):
                 act[c, g] = sb.tile([P, TILES, MM_N], F32, name="act%d%d" % (c, g))
                 for t in range(TILES):
                     nc.scalar.activation(
-                        out=act[c, g][:, t, :], in_=y_bank[c, g][:, chunks[t]], func=ACT.Tanh,
+                        out=act[c, g][:, t, :], in_=y_bank[c, g][:, y_cols[t]], func=ACT.Tanh,
                         bias=ob_sb[:, TILES * g + t, 0:1],
                     )
 
-        def finish(c):
-            for g in range(G):
-                res = sb.tile([P, TILES, MM_N], F32, name="res%d%d" % (c, g))
-                for t in range(TILES):
-                    nc.vector.tensor_scalar_mul(
-                        out=res[:, t, :], in0=act[c, g][:, t, :], scalar1=osc_sb[:, TILES * g + t, 0:1]
-                    )
-                nc.sync.dma_start(out=out[g].rearrange("(t q) n -> q t n", t=TILES)[:, :, chunks[c]], in_=res[:])
+        def finish(c, g):
+            res = sb.tile([P, TILES, MM_N], F32, name="res%d%d" % (c, g))
+            for t in range(TILES):
+                nc.vector.tensor_scalar_mul(
+                    out=res[:, t, :], in0=act[c, g][:, t, :], scalar1=osc_sb[:, TILES * g + t, 0:1]
+                )
+            nc.sync.dma_start(out=out[g].rearrange("(t q) n -> q t n", t=TILES)[:, :, chunks[c]], in_=res[:])
 
-        for c in range(CHUNKS + 2):
+        for c in range(CHUNKS + FINISH_LAG):
             if c < CHUNKS:
                 pack_words(c)
-                second_product(c)
-                activate(c)
-            if c >= 2:
-                finish(c - 2)
+            if c == 0:
+                wo2_q = quantize("wo2", wo2_grouped, K)
+            if c >= FINISH_LAG:
+                finish(c - FINISH_LAG, 0)
+            if c < CHUNKS:
+                second_layer(c, wo2_q)
+            if c >= FINISH_LAG:
+                finish(c - FINISH_LAG, 1)

import math
from contextlib import ExitStack

import concourse.mybir as mybir

F32 = mybir.dt.float32
BF16 = mybir.dt.bfloat16
U32 = mybir.dt.uint32
U8 = mybir.dt.uint8
FP8X4 = mybir.dt.float8_e4m3fn_x4
ACT = mybir.ActivationFunctionType
ALU = mybir.AluOpType

G = 2
K = 256
N = 512
P = 128
PACK = 4
ROWS = K // PACK
TILES = K // P
HALVES = 2
HALF = N // HALVES
MM_N = 128
CHUNKS = N // MM_N
LINE = 4
LINES = K // LINE
VECTOR_LINES = 42
FINISH_LAG = 2
PAD = 8
KNEE = 32.0

FLOPS = 3 * 2 * G * K * K * N


def tile_rows_frowshare_kernel(tc, x, w1, w2, reserve, hs, wo2, ob, osc, out):
    nc = tc.nc

    with ExitStack() as ctx:
        sb = ctx.enter_context(tc.tile_pool(name="sb", bufs=1))
        ps = ctx.enter_context(tc.psum_pool(name="ps", bufs=1))
        ctx.enter_context(tc.manual_schedule())
        ctx.enter_context(nc.allow_non_contiguous_dma(reason="ob and osc: one value a partition"))

        def packed_rows(src):
            return src.rearrange("g (p j) c -> (g p) j c", j=PACK)

        def load_rows(name, src):
            raw = sb.tile([P, PACK, src.shape[2]], F32, name=name + "_raw", align_bytes=64)
            nc.sync.dma_start(out=raw[:], in_=src)
            return raw

        def load_per_feature(name, src):
            vec = sb.tile([P, G, PAD], F32, name=name + "_sb")
            nc.sync.dma_start(out=vec[:, :, 0:TILES], in_=src.rearrange("g (q t) o -> q g (t o)", t=TILES))
            return vec

        def load_per_output(name, src):
            vec = sb.tile([P, G * TILES, PAD], F32, name=name + "_sb")
            nc.sync.dma_start(out=vec[:, :, 0:1], in_=src.rearrange("g (t q) o -> q (g t) o", t=TILES))
            return vec

        def quantize(name, grouped, width):
            codes = sb.tile([P, width], U32, name=name + "_codes", align_bytes=64)
            scales = sb.tile([P, width], U8, name=name + "_scales", align_bytes=64)
            nc.vector.quantize_mx(out=codes[:].bitcast(FP8X4), scales=scales[:], in_=grouped[:])
            return codes, scales

        def interleave(dst, src, vector_lines):
            nc.vector.tensor_copy(out=dst[:, 0:vector_lines], in_=src[:, 0:vector_lines])
            if vector_lines < LINES:
                nc.scalar.copy(out=dst[:, vector_lines:], in_=src[:, vector_lines:])

        def deal_weights(name, raw, vector_lines):
            grouped = sb.tile([P, K * PACK], BF16, name=name + "_grouped", align_bytes=64)
            interleave(
                grouped[:].rearrange("p (t c r j) -> p c j r t", t=TILES, r=LINE // TILES, j=PACK),
                raw[:].rearrange("p j (c r t) -> p c j r t", r=LINE // TILES, t=TILES),
                vector_lines,
            )
            return grouped

        def multiply(acc, g, t, weights, moving, width):
            rows = slice(ROWS * g, ROWS * (g + 1))
            w_cols = slice(P * t, P * (t + 1))
            for n0 in range(0, width, MM_N):
                cols = slice(n0, n0 + MM_N)
                nc.tensor.matmul_mx(
                    out=acc[:, cols],
                    lhsT=weights[0][rows, w_cols].bitcast(FP8X4),
                    lhsT_scale=weights[1][rows, w_cols],
                    rhs=moving[0][rows, cols].bitcast(FP8X4),
                    rhs_scale=moving[1][rows, cols],
                    start=True,
                    stop=True,
                )

        halves = [slice(HALF * h, HALF * (h + 1)) for h in range(HALVES)]
        chunks = [slice(MM_N * c, MM_N * (c + 1)) for c in range(CHUNKS)]
        gt = [(g, t) for g in range(G) for t in range(TILES)]
        hg = [(h, g) for h in range(HALVES) for g in range(G)]
        cg = [(c, g) for c in range(CHUNKS) for g in range(G)]

        w1_raw = load_rows("w1", packed_rows(w1))
        x_raw = [load_rows("x%d" % h, packed_rows(x)[:, :, halves[h]]) for h in range(HALVES)]
        w2_raw = load_rows("w2", packed_rows(w2))
        re_sb = load_per_feature("re", reserve)
        hs_sb = load_per_feature("hs", hs)
        wo2_raw = load_rows("wo2", packed_rows(wo2))
        ob_sb = load_per_output("ob", ob)
        osc_sb = load_per_output("osc", osc)

        bank_a = {(g, i): ps.tile([P, N], F32, name="bank_a%d%d" % (g, i)) for g, i in gt}
        bank_b = {(g, i): ps.tile([P, N], F32, name="bank_b%d%d" % (g, i)) for g, i in gt}

        w1_q = quantize("w1", deal_weights("w1", w1_raw, VECTOR_LINES), K)
        x_q = []
        expz = {(g, t): sb.tile([P, N], F32, name="expz%d%d" % (g, t)) for g, t in gt}
        for h in range(HALVES):
            x_grouped = sb.tile([P, HALF * PACK], BF16, name="x%d_grouped" % h, align_bytes=64)
            interleave(
                x_grouped[:].rearrange("p (c i j) -> p c j i", i=LINE, j=PACK),
                x_raw[h][:].rearrange("p j (c i) -> p c j i", i=LINE),
                VECTOR_LINES if h == 0 else LINES,
            )
            x_q.append(quantize("x%d" % h, x_grouped, HALF))
            for g, t in gt:
                multiply(bank_a[g, t][:, halves[h]], g, t, w1_q, x_q[h], HALF)
            for g, t in gt:
                nc.scalar.activation(out=expz[g, t][:, halves[h]], in_=bank_a[g, t][:, halves[h]], func=ACT.Exp)

        w2_q = quantize("w2", deal_weights("w2", w2_raw, LINES), K)
        for h, g in hg:
            for t in range(TILES):
                multiply(bank_b[g, h][:, HALF * t : HALF * (t + 1)], g, t, w2_q, x_q[h], HALF)

        capped = {(g, t): sb.tile([P, N], F32, name="capped%d%d" % (g, t)) for g, t in gt}
        stretch = {(g, t): sb.tile([P, N], F32, name="stretch%d%d" % (g, t)) for g, t in gt}
        logs = {(g, t): sb.tile([P, N], F32, name="logs%d%d" % (g, t)) for g, t in gt}
        excess = [sb.tile([P, TILES], F32, name="excess%d" % g) for g in range(G)]
        base = [sb.tile([P, TILES], F32, name="base%d" % g) for g in range(G)]
        sums = {(g, t): sb.tile([P, 1], F32, name="sums%d%d" % (g, t)) for g, t in gt}
        zs = {(g, t): sb.tile([P, 1], F32, name="zs%d%d" % (g, t)) for g, t in gt}
        factor = {(g, t): sb.tile([P, 1], F32, name="factor%d%d" % (g, t)) for g, t in gt}
        hs_inv = sb.tile([P, G, TILES], F32, name="hs_inv")
        share = [sb.tile([P, TILES, N], F32, name="share%d" % g) for g in range(G)]

        for g, t in gt:
            nc.vector.tensor_scalar(
                out=stretch[g, t][:], in0=bank_a[g, t][:], scalar1=KNEE, scalar2=-N * KNEE,
                op0=ALU.max, op1=ALU.add, accum_out=excess[g][:, t : t + 1],
            )
            nc.gpsimd.tensor_scalar(
                out=capped[g, t][:], in0=expz[g, t][:], scalar1=math.exp(KNEE), scalar2=0.0,
                op0=ALU.min, op1=ALU.max,
            )

        wo2_grouped = sb.tile([P, K * PACK], BF16, name="wo2_grouped", align_bytes=64)
        nc.vector.tensor_copy(
            out=wo2_grouped[:].rearrange("p (c i j) -> p c j i", i=LINE, j=PACK)[:, 0 : P // LINE],
            in_=wo2_raw[:].rearrange("p j (c i) -> p c j i", i=LINE)[:, 0 : P // LINE],
        )
        nc.gpsimd.tensor_scalar(
            out=wo2_grouped[:].rearrange("p (o j) -> p o j", j=PACK)[:, P:, :],
            in0=wo2_raw[:].rearrange("p j o -> p o j")[:, P:, :],
            scalar1=1.0, scalar2=0.0, op0=ALU.mult, op1=ALU.add,
        )
        nc.vector.reciprocal(out=hs_inv[:], in_=hs_sb[:, :, 0:TILES])
        for g in range(G):
            nc.vector.tensor_tensor(out=base[g][:], in0=excess[g][:], in1=re_sb[:, g, 0:TILES], op=ALU.add)

        for g, t in gt:
            nc.scalar.activation(
                out=logs[g, t][:], in_=capped[g, t][:], func=ACT.Ln, bias=1.0, accum_out=sums[g, t][:]
            )
        gate = {}
        for c, g in cg:
            h, part = divmod(c, CHUNKS // HALVES)
            gate[c, g] = sb.tile([P, MM_N, TILES], F32, name="gate%d%d" % (c, g))
            nc.scalar.activation(
                out=gate[c, g][:],
                in_=bank_b[g, h][:].rearrange("p (t n) -> p n t", t=TILES)[:, chunks[part], :],
                func=ACT.Tanh,
            )

        def total(g, t):
            nc.vector.tensor_scalar(
                out=zs[g, t][:], in0=sums[g, t][:], scalar1=base[g][:, t : t + 1],
                scalar2=hs_inv[:, g, t : t + 1], op0=ALU.add, op1=ALU.mult,
            )

        def invert(g, t):
            nc.vector.reciprocal(out=factor[g, t][:], in_=zs[g, t][:])

        def normalise(g, t):
            nc.vector.scalar_tensor_tensor(
                out=share[g][:, t, :], in0=logs[g, t][:], scalar=factor[g, t][:],
                in1=stretch[g, t][:], op0=ALU.mult, op1=ALU.mult,
            )

        total(*gt[0])
        invert(*gt[0])
        for this, following in zip(gt, gt[1:]):
            total(*following)
            normalise(*this)
            invert(*following)
        normalise(*gt[-1])

        gathered = [
            sb.tile([P, P // ROWS, MM_N * TILES], BF16, name="gathered%d" % c, align_bytes=64) for c in range(CHUNKS)
        ]
        for c, g in cg:
            pairs = sb.tile([P, MM_N * TILES], BF16, name="pairs%d%d" % (c, g), align_bytes=64)
            nc.vector.scalar_tensor_tensor(
                out=pairs[:].rearrange("p (n t) -> p n t", t=TILES),
                in0=share[g][:, :, chunks[c]].rearrange("p t n -> p n t"), scalar=N / KNEE,
                in1=gate[c, g][:], op0=ALU.mult, op1=ALU.mult,
            )
            nc.sync.dma_start(out=gathered[c][ROWS * g : ROWS * (g + 1), :, :], in_=pairs[:])

        y_bank = {(c, g): [bank_a, bank_b][c // TILES][g, c % TILES] for c, g in cg}
        y_cols = [slice(MM_N * t, MM_N * (t + 1)) for t in range(TILES)]
        hh_grouped = {}
        act = {}

        def pack_words(c):
            hh_grouped[c] = sb.tile([P, MM_N * PACK], BF16, name="hh%d_grouped" % c, align_bytes=64)
            nc.vector.tensor_copy(
                out=hh_grouped[c][:].bitcast(F32).rearrange("p (n u) -> p n u", u=P // ROWS),
                in_=gathered[c][:].bitcast(F32).rearrange("p u n -> p n u"),
            )

        def second_layer(c, wo2_q):
            hh_q = quantize("hh%d" % c, hh_grouped[c], MM_N)
            for g, t in gt:
                multiply(y_bank[c, g][:, y_cols[t]], g, t, wo2_q, hh_q, MM_N)
            for g in range(G):
                act[c, g] = sb.tile([P, TILES, MM_N], F32, name="act%d%d" % (c, g))
                for t in range(TILES):
                    nc.scalar.activation(
                        out=act[c, g][:, t, :], in_=y_bank[c, g][:, y_cols[t]], func=ACT.Tanh,
                        bias=ob_sb[:, TILES * g + t, 0:1],
                    )

        def finish(c, g):
            res = sb.tile([P, TILES, MM_N], F32, name="res%d%d" % (c, g))
            for t in range(TILES):
                nc.vector.tensor_scalar_mul(
                    out=res[:, t, :], in0=act[c, g][:, t, :], scalar1=osc_sb[:, TILES * g + t, 0:1]
                )
            nc.sync.dma_start(out=out[g].rearrange("(t q) n -> q t n", t=TILES)[:, :, chunks[c]], in_=res[:])

        for c in range(CHUNKS + FINISH_LAG):
            if c < CHUNKS:
                pack_words(c)
            if c == 0:
                wo2_q = quantize("wo2", wo2_grouped, K)
            if c >= FINISH_LAG:
                finish(c - FINISH_LAG, 0)
            if c < CHUNKS:
                second_layer(c, wo2_q)
            if c >= FINISH_LAG:
                finish(c - FINISH_LAG, 1)
